import numpy as np, ml_dtypes
CORES = [3,7,11,15,131,135,139,143]
N = 8
W, KW, DIL = 512, 5, 1
H = (KW // 2) * DIL
def setup_inputs(rng):
    return {"x": rng.standard_normal((N, 128, W), dtype=np.float32).astype(ml_dtypes.bfloat16), "w": rng.standard_normal((N, 128, KW * 128), dtype=np.float32).astype(ml_dtypes.bfloat16)}
def setup_inputs_big(rng):
    d = setup_inputs(rng)
    for k in ("x", "w"): d[k] = (d[k].astype(np.float32) * 1024.0).astype(d[k].dtype)
    return d
def setup_inputs_small(rng):
    d = setup_inputs(rng)
    for k in ("x", "w"): d[k] = (d[k].astype(np.float32) * (1 / 1024.0)).astype(d[k].dtype)
    return d
def reference(x, w):
    X, W_ = x.astype(np.float64), w.astype(np.float64)
    g = np.concatenate(list(X), axis=1)
    p = np.concatenate([g[:, -H:], g, g[:, :H]], axis=1)
    y = np.zeros((N, 128, W))
    for r in range(N):
        for i in range(KW):
            y[r] += W_[r][:, 128 * i:128 * i + 128].T @ p[:, W * r + i * DIL:W * r + i * DIL + W]
    return {"y": y.astype(ml_dtypes.bfloat16 if x.dtype != np.float64 else np.float64)}

from concourse.bass import DstId, RemoteDMATransfer

W, KW, HALO, CH = 512, 5, 2, 128
EDGE = 64
MID = [(EDGE, 192), (EDGE + 192, 192)]
N_ENG = 4

SCRATCH = {
    "xs": ("sbuf", [CH, W + 2 * HALO], "bfloat16"),
    "ws": ("sbuf", [CH, KW * CH], "bfloat16"),
    "ys": ("sbuf", [CH, W], "bfloat16"),
    "pm0": ("psum", [CH, 512], "float32"),
    "pm1": ("psum", [CH, 512], "float32"),
    "pl": ("psum", [CH, 512], "float32"),
    "pr": ("psum", [CH, 512], "float32"),
}
SEMAPHORES = ["el", "er", "xm", "wl", "hl", "hr", "sent",
              "mm0", "mm1", "ml", "mr", "cm0", "cm1", "cl", "cr", "stored"]


def _hops(topo, a, b):
    if topo.host(a) == topo.host(b) and topo.chip(a) == topo.chip(b):
        return 0
    return 1 if (topo.mates(a, b) or topo.same_plane(a, b)) else 2


def _take(mask, n, used):
    out, k, bit = 0, 0, 1
    while k < n:
        if mask & bit and not used & bit:
            out |= bit
            k += 1
        bit <<= 1
    return out


def rank_program(g, core, T, topo):
    rank = T.rank_of(core)
    if rank is None:
        return
    n = len(T.cores)
    left, right = T.cores[(rank - 1) % n], T.cores[(rank + 1) % n]
    S = T.sem
    xs, ws, ys = T.xs, T.ws, T.ys
    X0, X1 = HALO, HALO + W

    g.sync.dma_start(xs[:, X0:X0 + HALO], T.x[:, 0:HALO]).then_inc(S.el, 16)
    g.scalar.dma_start(xs[:, X1 - HALO:X1], T.x[:, W - HALO:W]).then_inc(S.er, 16)
    g.scalar.dma_start(ws[:, :], T.w[:, :]).then_inc(S.wl, 16)
    g.sync.dma_start(xs[:, X0 + HALO:X1 - HALO], T.x[:, HALO:W - HALO]).then_inc(S.xm, 16)

    sends = [(left, xs[:, X0:X0 + HALO], xs[:, X1:X1 + HALO], S.hr),
             (right, xs[:, X1 - HALO:X1], xs[:, 0:HALO], S.hl)]
    sends.sort(key=lambda s: -_hops(topo, core, s[0]))
    used, transfers = 0, []
    for dst, src_ap, dst_ap, sem in sends:
        rid, pid = topo.addr(dst, core)
        m = _take(topo.mask(core, dst), N_ENG, used)
        used |= m
        transfers.append(RemoteDMATransfer(dst_ids=[DstId(rid=rid, pnc=pid)], dma_engine_mask=m, remote_sem=sem,
                                           src=src_ap, dst=dst_ap))
    g.wait_ge(S.el, 16)
    g.wait_ge(S.er, 16)
    g.remote_dma_fused(transfers, local_sem=S.sent)

    t = g.tensor

    def mm(bank, c0, width, tap, start, stop):
        return t.matmul(bank[:, 0:width], ws[:, tap * CH:(tap + 1) * CH], xs[:, c0 + tap:c0 + tap + width],
                        start=start, stop=stop)

    t.wait_ge(S.wl, 16)
    t.wait_ge(S.xm, 16)
    for k, (c0, width) in enumerate(MID):
        for tap in range(KW):
            ins = mm(T["pm%d" % k], c0, width, tap, tap == 0, tap == KW - 1)
        ins.then_inc(S["mm%d" % k], 1)
    ends = [(T.pl, 0, [2, 3, 4], [0, 1], S.hl, S.ml, S.cl, left),
            (T.pr, W - EDGE, [2, 1, 0], [3, 4], S.hr, S.mr, S.cr, right)]
    ends.sort(key=lambda e: _hops(topo, e[7], core))
    t.wait_ge(S.el, 16)
    t.wait_ge(S.er, 16)
    for bank, c0, own, halo, hs, ms, cs, snd in ends:
        for k, tap in enumerate(own):
            mm(bank, c0, EDGE, tap, k == 0, False)
    for bank, c0, own, halo, hs, ms, cs, snd in ends:
        t.wait_ge(hs, N_ENG)
        mm(bank, c0, EDGE, halo[0], False, False)
        mm(bank, c0, EDGE, halo[1], False, True).then_inc(ms, 1)

    v = g.vector
    stores = 0
    for k, (c0, width) in enumerate(MID):
        v.wait_ge(S["mm%d" % k], 1)
        v.tensor_copy(ys[:, c0:c0 + width], T["pm%d" % k][:, 0:width]).then_inc(S["cm%d" % k], 1)
        g.sync.wait_ge(S["cm%d" % k], 1)
        g.sync.dma_start(T.y[:, c0:c0 + width], ys[:, c0:c0 + width]).then_inc(S.stored, 16)
        stores += 1
    for bank, c0, own, halo, hs, ms, cs, snd in ends:
        v.wait_ge(ms, 1)
        v.tensor_copy(ys[:, c0:c0 + EDGE], bank[:, 0:EDGE]).then_inc(cs, 1)
        g.scalar.wait_ge(cs, 1)
        g.scalar.dma_start(T.y[:, c0:c0 + EDGE], ys[:, c0:c0 + EDGE]).then_inc(S.stored, 16)
        stores += 1

    g.wait_ge(S.sent, 2 * N_ENG)
    g.wait_ge(S.stored, 16 * stores)
